import numpy as np
import ml_dtypes


def mxq(x, axis, fmt="e4m3"):
    dtype, down = {"e4m3": (ml_dtypes.float8_e4m3fn, 7), "e5m2": (ml_dtypes.float8_e5m2, 14)}[fmt]
    v = np.moveaxis(np.asarray(x, np.float32).astype(ml_dtypes.bfloat16).astype(np.float64), axis, -1)
    blocks = v.reshape(v.shape[:-1] + (-1, 32))
    amax = np.abs(blocks).max(-1, keepdims=True)
    byte = np.maximum(np.where(amax > 0, np.frexp(amax)[1] - 1 + 127, 0) - down, 1)
    scale = np.exp2(byte - 127.0)
    codes = (blocks / scale).astype(np.float32).astype(dtype).astype(np.float64)
    return np.moveaxis((codes * scale).reshape(v.shape), -1, axis)


WIDE = False


def mx_kscale(k):
    if not WIDE:
        return np.ones(k)
    levels = np.array([10, -10, 5, -5, 0])
    if k % 512:
        return np.exp2(np.random.permutation(np.resize(levels, k // 32))).repeat(32)
    a = np.empty((k // 512, 16))
    for p in range(k // 512):
        a[p, :8] = np.random.permutation(np.resize(levels, 8))
        for g in range(8):
            far = levels[np.abs(levels - a[p, g]) >= 10]
            a[p, g + 8] = far[np.random.randint(len(far))]
    return np.exp2(a.ravel()).repeat(32)


def f64(x):
    return np.asarray(x).astype(np.float64)


def striped(idx):
    return np.tile(np.asarray(idx).reshape(-1, 16).T, (8, 1)).astype(np.uint16)


def unstriped(offs):
    return offs[:16].T.reshape(-1).astype(np.int64)


E2M1 = np.array([0.0, 0.5, 1.0, 1.5, 2.0, 3.0, 4.0, 6.0, -0.0, -0.5, -1.0, -1.5, -2.0, -3.0, -4.0, -6.0])


def pack_weight(w, fmt):
    k, n = w.shape
    w = f64(np.asarray(w, np.float32).astype(ml_dtypes.bfloat16)).reshape(k // 32, 32, n)
    amax = np.abs(w).max(1)
    if fmt == "e4m3":
        byte = np.frexp(amax)[1] - 1 + 127 - 7
    else:
        mant, ex = np.frexp(amax / 6.0)
        byte = np.where(mant > 0.5, ex, ex - 1) + 127
    byte = np.clip(np.where(amax > 0, byte, 1), 1, 254)
    scaled = (w * np.exp2(127.0 - byte)[:, None, :]).reshape(k, n).astype(np.float32)
    by_word = np.ascontiguousarray(scaled.reshape(k // 512, 128, 4, n).transpose(0, 1, 3, 2))
    if fmt == "e4m3":
        words = by_word.astype(ml_dtypes.float8_e4m3fn).view(np.uint8)
    else:
        c = by_word.astype(ml_dtypes.float4_e2m1fn).view(np.uint8) & 0xF
        words = (c[..., 0::2] | (c[..., 1::2] << 4)).reshape(k // 512, 128, 2 * n)
    return np.ascontiguousarray(words), np.ascontiguousarray(byte.astype(np.uint8).reshape(k // 512, 16, n))


def unpack_weight(words, scales, fmt):
    g, _, n = scales.shape
    words = np.ascontiguousarray(words).reshape(g, 128, n, -1)
    if fmt == "e4m3":
        vals = words.view(ml_dtypes.float8_e4m3fn).astype(np.float64)
    else:
        nib = np.empty((g, 128, n, 4), np.uint8)
        nib[..., 0::2] = words & 0xF
        nib[..., 1::2] = words >> 4
        vals = E2M1[nib]
    vals = vals * np.repeat(np.exp2(scales.astype(np.float64) - 127.0), 8, axis=1)[..., None]
    return vals.transpose(0, 1, 3, 2).reshape(g * 512, n)


def bf(x):
    return np.asarray(x, np.float32).astype(ml_dtypes.bfloat16)


def planes(Y):
    r, m = Y.shape
    b = f64(bf(Y)).reshape(r // 32, 32, m)
    amax = np.abs(b).max(1)
    byte = np.clip(np.where(amax > 0, np.frexp(amax)[1] - 1 + 127 - 7, 1), 1, 254)
    codes = (b * np.exp2(127.0 - byte)[:, None, :]).reshape(r, m).astype(np.float32).astype(ml_dtypes.float8_e4m3fn).view(np.uint8)
    words = codes.reshape(r // 512, 128, 4, m).transpose(0, 1, 3, 2)
    return np.ascontiguousarray(words), np.ascontiguousarray(byte.astype(np.uint8).reshape(r // 512, 16, m))


K, T, J, I, N = 1024, 1024, 512, 512, 512


def setup_inputs():
    n = np.random.standard_normal
    idx = np.random.permutation(T)[:J]
    idx2 = np.random.permutation(T)[:I]
    fk = mx_kscale(K)
    xqp = pack_weight(n((K, T)) / fk[:, None], "e2m1")
    wsp = pack_weight(n((K, N)) * 1 / np.sqrt(K) * fk[:, None], "e4m3")
    wbp = pack_weight(n((K, N)) * 1 / np.sqrt(K) * fk[:, None], "e4m3")
    return {
        "xq_words": xqp[0],
        "xq_scales": xqp[1],
        "ws_words": wsp[0],
        "ws_scales": wsp[1],
        "wa": (n((K, N)) * 1 / np.sqrt(K) * fk[:, None]).astype(np.float32),
        "wb_words": wbp[0],
        "wb_scales": wbp[1],
        "ga": (np.random.uniform(0.2, 0.9, (1, J))).astype(np.float32),
        "gb": (np.random.uniform(0.2, 0.9, (1, I))).astype(np.float32),
        "offs": striped(idx),
        "offs2": striped(idx2),
    }


def reference(xq_words, xq_scales, ws_words, ws_scales, wa, wb_words, wb_scales, ga, gb, offs, offs2):
    idx = unstriped(offs)
    idx2 = unstriped(offs2)
    xqu = unpack_weight(xq_words, xq_scales, "e2m1")
    wsu = unpack_weight(ws_words, ws_scales, "e4m3")
    wbu = unpack_weight(wb_words, wb_scales, "e4m3")
    s = wsu.T @ xqu
    waq = mxq(f64(wa), 0, "e4m3")
    xqidxg = xqu[:, idx]
    p = waq.T @ xqidxg
    xqidx2g = xqu[:, idx2]
    q = wbu.T @ xqidx2g
    pw = p * f64(ga)
    qw = q * f64(gb)
    pg = np.zeros((N, T))
    pg[:, idx] = pw
    qg = np.zeros((N, T))
    qg[:, idx2] = qw
    y = s + pg + qg
    words, scales = planes(y)
    return y, words, scales

@@ -1,0 +1,246 @@
+from contextlib import ExitStack
+
+import concourse.mybir as mybir
+from concourse.masks import make_identity
+
+K, T, J, N = 1024, 1024, 512, 512
+FLOPS = 2 * K * N * (T + 2 * J)
+
+F32 = mybir.dt.float32
+BF16 = mybir.dt.bfloat16
+I32 = mybir.dt.int32
+U16 = mybir.dt.uint16
+U8 = mybir.dt.uint8
+FP8X4 = mybir.dt.float8_e4m3fn_x4
+FP4X4 = mybir.dt.float4_e2m1fn_x4
+MULT = mybir.AluOpType.mult
+ADD = mybir.AluOpType.add
+
+P = 128
+PACK = 4
+PASSES = K // 512
+BANK = 512
+HALVES = T // BANK
+CHUNK = 256
+CHUNKS = T // CHUNK
+LIVE = 100
+
+
+def tile_list_experts_shared_pl_kernel(tc, xq_words, xq_scales, ws_words, ws_scales, wa, wb_words, wb_scales,
+                                           ga, gb, offs, offs2, out_0, out_1, out_2):
+    nc = tc.nc
+    with ExitStack() as ctx:
+        lists = ctx.enter_context(tc.tile_pool(name="lists", bufs=1))
+        sb = ctx.enter_context(tc.tile_pool(name="sb", bufs=1))
+        ps = ctx.enter_context(tc.psum_pool(name="ps", bufs=1))
+
+        def tile(shape, dtype, name, tag=None):
+            return sb.tile(shape, dtype, name=name, tag=tag or name, align_bytes=64)
+
+        def zero_bytes(engine, plane):
+            engine.memset(plane.bitcast(I32), 0)
+
+        list_a = lists.tile([P, J // 16], U16, name="list_a")
+        list_b = lists.tile([P, J // 16], U16, name="list_b")
+
+        x_words = [tile([P, T], U16, f"x_words{z}") for z in range(PASSES)]
+        x_scales = tile([P, T], U8, "x_scales")
+        x_scales1 = tile([P, T], U8, "x_scales1")
+        wb_raw = tile([P, PASSES, N], I32, "wb_raw")
+        wb_raw_scales = tile([P, PASSES, N], U8, "wb_raw_scales")
+        wb_codes = tile([P, PASSES, PACK, P], I32, "wb_codes")
+        wb_planes = tile([P, PASSES, PACK, P], U8, "wb_planes")
+        ws_codes = tile([P, PASSES, N], I32, "ws_codes")
+        ws_planes = tile([P, PASSES, N], U8, "ws_planes")
+        wa_raw = [[tile([P, PACK, N // 2], F32, f"wa_raw{z}{u}") for u in range(2)] for z in range(PASSES)]
+        wa_bf = tile([P, PASSES, PACK, P, PACK], BF16, "wa_bf")
+        wa_codes = tile([P, PASSES, PACK, P], I32, "wa_codes")
+        wa_planes = tile([P, PASSES, PACK, P], U8, "wa_planes")
+        picked = {e: [tile([P, J], U16, f"picked_{e}{z}") for z in range(PASSES)] for e in "ab"}
+        picked_scales = {e: tile([P, J], U8, f"picked_scales_{e}") for e in "ab"}
+        picked_scales1 = {e: tile([P, J], U8, f"picked_scales1_{e}") for e in "ab"}
+        gate_cols = {e: tile([P, PACK], F32, f"gate_cols_{e}") for e in "ab"}
+        gates = {e: tile([P, J], F32, f"gates_{e}") for e in "ab"}
+        ident = tile([P, P], F32, "ident")
+        page_b = [tile([P, T], F32, f"page_b{i}") for i in range(2)]
+        first_src = tile([P, J], F32, "first_src")
+        src_ring = [tile([P, J], F32, f"src_ring{i}") for i in range(2)]
+        shared_t = [tile([P, PACK, P], F32, f"shared_t{b}") for b in range(T // P)]
+        pages_t = [[tile([P, BANK], F32, f"pages_t{i}{h}") for h in range(HALVES)] for i in range(2)]
+        y_pairs = [[tile([P, 2, BANK], F32, f"y{u}{h}") for h in range(HALVES)] for u in range(2)]
+        y_bf = [tile([P, CHUNK, PACK], BF16, f"y_bf{c}") for c in range(CHUNKS)]
+        y_codes = [tile([P, CHUNK], I32, f"y_codes{c}") for c in range(CHUNKS)]
+        y_planes = tile([P, T], U8, "y_planes")
+
+        expert_banks = [ps.tile([P, BANK], F32, name=f"expert_bank{i}") for i in range(2)]
+        shared_banks = [ps.tile([P, BANK], F32, name=f"shared_bank{i}") for i in range(2)]
+        turn_banks = [ps.tile([P, BANK], F32, name=f"turn_bank{h}") for h in range(HALVES)]
+        y_banks = [ps.tile([P, BANK], F32, name=f"y_bank{h}") for h in range(HALVES)]
+
+        zero_bytes(nc.vector, x_scales[:])
+        zero_bytes(nc.vector, wb_raw_scales[:].rearrange("p z n -> p (z n)"))
+        zero_bytes(nc.vector, picked_scales1["b"][:])
+        for page in page_b:
+            nc.vector.memset(page[:], 0.0)
+        make_identity(nc, ident[:])
+        zero_bytes(nc.gpsimd, picked_scales1["a"][:])
+        zero_bytes(nc.gpsimd, ws_planes[:].rearrange("p z n -> p (z n)"))
+        zero_bytes(nc.gpsimd, x_scales1[:])
+
+        def load_planes(plane, scales):
+            for q in range(4):
+                nc.sync.dma_start(out=plane[32 * q:32 * q + 4, :, :].bitcast(I32),
+                                  in_=scales[:, 4 * q:4 * q + 4, :].rearrange("z r n -> r z n").bitcast(I32))
+
+        nc.sync.dma_start(list_b[:], offs2)
+        for q in range(4):
+            nc.sync.dma_start(out=x_scales[32 * q:32 * q + 8, :].bitcast(I32),
+                              in_=xq_scales[:, 4 * q:4 * q + 4, :].bitcast(I32))
+        for z in range(PASSES):
+            nc.sync.dma_start(out=x_words[z][:].bitcast(I32), in_=xq_words[z].bitcast(I32))
+        nc.sync.dma_start(out=wb_raw[:], in_=wb_words.rearrange("z p n t -> p z (n t)").bitcast(I32))
+        load_planes(wb_raw_scales, wb_scales)
+        nc.sync.dma_start(list_a[:], offs)
+        nc.sync.dma_start(out=gate_cols["b"][:], in_=gb.rearrange("o (p c) -> (o p) c", c=PACK))
+        for z in range(PASSES):
+            rows = wa[512 * z:512 * (z + 1), :].rearrange("(p j) n -> p j n", j=PACK)
+            for u in range(2):
+                nc.sync.dma_start(out=wa_raw[z][u][:], in_=rows[:, :, 256 * u:256 * (u + 1)])
+        nc.sync.dma_start(out=gate_cols["a"][:], in_=ga.rearrange("o (p c) -> (o p) c", c=PACK))
+        nc.sync.dma_start(out=ws_codes[:], in_=ws_words.rearrange("z p n t -> p z (n t)").bitcast(I32))
+        load_planes(ws_planes, ws_scales)
+        nc.sync.dma_start(out=x_scales1[0:LIVE, :].bitcast(I32), in_=x_scales[4:4 + LIVE, :].bitcast(I32))
+
+        def gather(e, offsets, queue):
+            nc.vector.tensor_copy(picked_scales[e][:], x_scales[:].indirect(offsets[:]))
+            queue.dma_start(out=picked_scales1[e][0:LIVE, :].bitcast(I32),
+                            in_=picked_scales[e][4:4 + LIVE, :].bitcast(I32))
+            for z in range(PASSES):
+                nc.vector.tensor_copy(picked[e][z][:], x_words[z][:].indirect(offsets[:]))
+
+        def spread_gate(e, bank):
+            for c in range(PACK):
+                nc.tensor.transpose(bank[:, P * c:P * (c + 1)], gate_cols[e][:, c:c + 1].to_broadcast([P, P]), ident[:])
+            nc.scalar.copy(out=gates[e][:].rearrange("p (n c) -> p n c", c=PACK),
+                           in_=bank[:].rearrange("p (c n) -> p n c", c=PACK))
+
+        gather("b", list_b, nc.scalar)
+        nc.vector.tensor_copy(out=wb_codes[:].rearrange("p z r m -> p z m r"),
+                              in_=wb_raw[:].rearrange("p z (m r) -> p z m r", r=PACK))
+        nc.vector.tensor_copy(out=wb_planes[:].rearrange("p z r m -> p z m r"),
+                              in_=wb_raw_scales[:].rearrange("p z (m r) -> p z m r", r=PACK))
+        gather("a", list_a, nc.gpsimd)
+        spread_gate("b", y_banks[0])
+
+        def expert_product(e, r, bank, src):
+            codes, planes = (wa_codes, wa_planes) if e == "a" else (wb_codes, wb_planes)
+            for z in range(PASSES):
+                nc.tensor.matmul_mx(out=bank[:], lhsT=codes[:, z, r, :].bitcast(FP8X4), lhsT_scale=planes[:, z, r, :],
+                                    rhs=picked[e][z][:].bitcast(FP4X4),
+                                    rhs_scale=(picked_scales, picked_scales1)[z][e][:],
+                                    start=z == 0, stop=z == PASSES - 1)
+            nc.scalar.copy(out=src, in_=bank[:])
+
+        def scatter(e, page, src):
+            offsets = list_a if e == "a" else list_b
+            nc.vector.tensor_tensor(page[:].indirect(offsets[:]), src, gates[e][:], MULT)
+
+        def cast_wa(z, u):
+            nc.scalar.copy(out=wa_bf[:, z, :, 64 * u:64 * (u + 1), :].rearrange("p r m j -> p m j r"),
+                           in_=wa_raw[z][u][:].rearrange("p j (m r) -> p m j r", r=PACK))
+
+        def shared_product(b):
+            bank = (shared_banks + turn_banks)[b % 4]
+            for z in range(PASSES):
+                nc.tensor.matmul_mx(out=bank[:], lhsT=x_words[z][:, P * b:P * (b + 1)].bitcast(FP4X4),
+                                    lhsT_scale=(x_scales, x_scales1)[z][:, P * b:P * (b + 1)],
+                                    rhs=ws_codes[:, z, :].bitcast(FP8X4), rhs_scale=ws_planes[:, z, :],
+                                    start=z == 0, stop=z == PASSES - 1)
+            nc.scalar.copy(out=shared_t[b][:], in_=bank[:].rearrange("p (m r) -> p r m", r=PACK))
+
+        def add_turned(bank, blocks, start, stop):
+            for i, block in enumerate(blocks):
+                nc.tensor.matmul(bank[:, P * (i % 4):P * (i % 4 + 1)], lhsT=block, rhs=ident[:], is_transpose=True,
+                                 start=start and i == 0, stop=stop and i == len(blocks) - 1)
+
+        def page_blocks(page, h):
+            return [page[:, BANK * h + P * i:BANK * h + P * (i + 1)] for i in range(4)]
+
+        sum_banks = [y_banks, shared_banks]
+
+        def sum_on_tensor(r, pages):
+            turned, banks = pages_t[r % 2], sum_banks[r % 2]
+            for h in range(HALVES):
+                add_turned(banks[h], [shared_t[4 * h + i][:, r, :] for i in range(4)], True, False)
+            for h in range(HALVES):
+                add_turned(turn_banks[h], [b for page in pages for b in page_blocks(page, h)], True, True)
+                nc.scalar.copy(out=turned[h][:], in_=turn_banks[h][:])
+            for h in range(HALVES):
+                add_turned(banks[h], [turned[h][:, P * i:P * (i + 1)] for i in range(4)], False, True)
+
+        y_rows = out_0.rearrange("(p r) t -> r p t", r=PACK)
+
+        def store_y(r, h):
+            nc.sync.dma_start(out=y_rows[r][:, BANK * h:BANK * (h + 1)], in_=y_pairs[r // 2][h][:, r % 2, :])
+
+        def finish_slice(r, pages):
+            sum_on_tensor(r, pages)
+            for h in range(HALVES):
+                nc.scalar.copy(out=y_pairs[r // 2][h][:, r % 2, :], in_=sum_banks[r % 2][h][:])
+                store_y(r, h)
+
+        def cast_pair(copy, u, c):
+            h, c0 = divmod(c * CHUNK, BANK)
+            copy(out=y_bf[c][:, :, 2 * u:2 * u + 2],
+                 in_=y_pairs[u][h][:, :, c0:c0 + CHUNK].rearrange("p r t -> p t r"))
+
+        cast_wa(0, 0)
+        cast_wa(0, 1)
+        expert_product("b", 0, expert_banks[0], first_src[:])
+        scatter("b", page_b[0], first_src[:])
+        cast_wa(1, 0)
+        cast_wa(1, 1)
+        page_a = [tile([P, T], F32, "page_a0", tag="wa_raw01"), tile([P, T], F32, "page_a1", tag="wa_raw10")]
+        for page in page_a:
+            nc.gpsimd.memset(page[:], 0.0)
+        nc.vector.quantize_mx(out=wa_codes[:].rearrange("p z r m -> p (z r m)").bitcast(FP8X4),
+                              scales=wa_planes[:].rearrange("p z r m -> p (z r m)"),
+                              in_=wa_bf[:].rearrange("p z r m j -> p (z r m j)"))
+        second_src = wa_raw[1][1][:].rearrange("p j n -> p (j n)")[:, 0:J]
+        expert_product("b", 1, expert_banks[1], second_src)
+        scatter("b", page_b[1], second_src)
+        spread_gate("a", y_banks[1])
+        expert_product("a", 0, expert_banks[0], src_ring[0][:])
+        expert_product("a", 1, expert_banks[1], src_ring[1][:])
+        for b in range(T // P):
+            shared_product(b)
+        scatter("a", page_a[0], src_ring[0][:])
+        scatter("a", page_a[1], src_ring[1][:])
+        expert_product("b", 2, turn_banks[1], src_ring[0][:])
+        finish_slice(0, [page_a[0], page_b[0]])
+        scatter("b", page_b[0], src_ring[0][:])
+        expert_product("a", 2, expert_banks[1], pages_t[0][1][:])
+        finish_slice(1, [page_a[1], page_b[1]])
+        scatter("a", page_a[0], pages_t[0][1][:])
+        expert_product("b", 3, expert_banks[0], pages_t[1][1][:])
+        for c in range(CHUNKS):
+            cast_pair(nc.scalar.copy, 0, c)
+        scatter("b", page_b[1], pages_t[1][1][:])
+        expert_product("a", 3, expert_banks[0], src_ring[1][:])
+        finish_slice(2, [page_a[0], page_b[0]])
+        scatter("a", page_a[1], src_ring[1][:])
+        sum_on_tensor(3, [page_b[1]])
+        for h in range(HALVES):
+            nc.vector.tensor_tensor(y_pairs[1][h][:, 1, :], sum_banks[1][h][:], page_a[1][:, BANK * h:BANK * (h + 1)], ADD)
+            store_y(3, h)
+        for c in range(CHUNKS):
+            cast_pair(nc.scalar.copy if c < 2 else nc.vector.tensor_copy, 1, c)
+        words = out_1[0].rearrange("p c t -> p (c t)").bitcast(I32)
+        for c in (0, 2, 1, 3):
+            nc.vector.quantize_mx(out=y_codes[c][:].bitcast(FP8X4), scales=y_planes[:, CHUNK * c:CHUNK * (c + 1)],
+                                  in_=y_bf[c][:].rearrange("p t r -> p (t r)"))
+            nc.sync.dma_start(out=words[:, CHUNK * c:CHUNK * (c + 1)], in_=y_codes[c][:])
+        for q in range(4):
+            queue = nc.scalar if q % 2 == 0 else nc.sync
+            queue.dma_start(out=out_2[0, 4 * q:4 * q + 4, :].bitcast(I32),
+                            in_=y_planes[32 * q:32 * q + 4, :].bitcast(I32))

@@ -58,15 +58,15 @@ def tile_list_experts_shared_pl_kernel(tc, xq_words, xq_scales, ws_words, ws_sca
         wa_planes = tile([P, PASSES, PACK, P], U8, "wa_planes")
         picked = {e: [tile([P, J], U16, f"picked_{e}{z}") for z in range(PASSES)] for e in "ab"}
         picked_scales = {e: tile([P, J], U8, f"picked_scales_{e}") for e in "ab"}
-        picked_scales1 = {e: tile([P, J], U8, f"picked_scales1_{e}") for e in "ab"}
+        picked_scales1 = {"a": tile([P, J], U8, "picked_scales1_a")}
         gate_cols = {e: tile([P, PACK], F32, f"gate_cols_{e}") for e in "ab"}
         gates = {e: tile([P, J], F32, f"gates_{e}") for e in "ab"}
         ident = tile([P, P], F32, "ident")
-        page_b = [tile([P, T], F32, f"page_b{i}") for i in range(2)]
-        first_src = tile([P, J], F32, "first_src")
-        src_ring = [tile([P, J], F32, f"src_ring{i}") for i in range(2)]
+        page_b = [tile([P, T], F32, "page_b0")]
+        src_a = [tile([P, J], F32, f"src_a{r}") for r in range(PACK)]
+        later_src_b = [tile([P, J], F32, f"src_b{r}") for r in range(1, PACK)]
         shared_t = [tile([P, PACK, P], F32, f"shared_t{b}") for b in range(T // P)]
-        pages_t = [[tile([P, BANK], F32, f"pages_t{i}{h}") for h in range(HALVES)] for i in range(2)]
+        turned = [tile([P, BANK], F32, f"turned{h}") for h in range(HALVES)]
         y_pairs = [[tile([P, 2, BANK], F32, f"y{u}{h}") for h in range(HALVES)] for u in range(2)]
         y_bf = [tile([P, CHUNK, PACK], BF16, f"y_bf{c}") for c in range(CHUNKS)]
         y_codes = [tile([P, CHUNK], I32, f"y_codes{c}") for c in range(CHUNKS)]
@@ -79,9 +79,9 @@ def tile_list_experts_shared_pl_kernel(tc, xq_words, xq_scales, ws_words, ws_sca
 
         zero_bytes(nc.vector, x_scales[:])
         zero_bytes(nc.vector, wb_raw_scales[:].rearrange("p z n -> p (z n)"))
-        zero_bytes(nc.vector, picked_scales1["b"][:])
-        for page in page_b:
-            nc.vector.memset(page[:], 0.0)
+        page_a = tile([P, T], F32, "page_a")
+        nc.vector.memset(page_b[0][:], 0.0)
+        nc.vector.memset(page_a[:], 0.0)
         make_identity(nc, ident[:])
         zero_bytes(nc.gpsimd, picked_scales1["a"][:])
         zero_bytes(nc.gpsimd, ws_planes[:].rearrange("p z n -> p (z n)"))
@@ -92,6 +92,7 @@ def tile_list_experts_shared_pl_kernel(tc, xq_words, xq_scales, ws_words, ws_sca
                 nc.sync.dma_start(out=plane[32 * q:32 * q + 4, :, :].bitcast(I32),
                                   in_=scales[:, 4 * q:4 * q + 4, :].rearrange("z r n -> r z n").bitcast(I32))
 
+        nc.sync.dma_start(out=gate_cols["b"][:], in_=gb.rearrange("o (p c) -> (o p) c", c=PACK))
         nc.sync.dma_start(list_b[:], offs2)
         for q in range(4):
             nc.sync.dma_start(out=x_scales[32 * q:32 * q + 8, :].bitcast(I32),
@@ -101,7 +102,6 @@ def tile_list_experts_shared_pl_kernel(tc, xq_words, xq_scales, ws_words, ws_sca
         nc.sync.dma_start(out=wb_raw[:], in_=wb_words.rearrange("z p n t -> p z (n t)").bitcast(I32))
         load_planes(wb_raw_scales, wb_scales)
         nc.sync.dma_start(list_a[:], offs)
-        nc.sync.dma_start(out=gate_cols["b"][:], in_=gb.rearrange("o (p c) -> (o p) c", c=PACK))
         for z in range(PASSES):
             rows = wa[512 * z:512 * (z + 1), :].rearrange("(p j) n -> p j n", j=PACK)
             for u in range(2):
@@ -124,13 +124,15 @@ def tile_list_experts_shared_pl_kernel(tc, xq_words, xq_scales, ws_words, ws_sca
             nc.scalar.copy(out=gates[e][:].rearrange("p (n c) -> p n c", c=PACK),
                            in_=bank[:].rearrange("p (c n) -> p n c", c=PACK))
 
+        spread_gate("b", y_banks[0])
+        picked_scales1["b"] = tile([P, J], U8, "picked_scales1_b", tag="gate_cols_b")
+        zero_bytes(nc.gpsimd, picked_scales1["b"][:])
         gather("b", list_b, nc.scalar)
         nc.vector.tensor_copy(out=wb_codes[:].rearrange("p z r m -> p z m r"),
                               in_=wb_raw[:].rearrange("p z (m r) -> p z m r", r=PACK))
         nc.vector.tensor_copy(out=wb_planes[:].rearrange("p z r m -> p z m r"),
                               in_=wb_raw_scales[:].rearrange("p z (m r) -> p z m r", r=PACK))
-        gather("a", list_a, nc.gpsimd)
-        spread_gate("b", y_banks[0])
+        gather("a", list_a, nc.sync)
 
         def expert_product(e, r, bank, src):
             codes, planes = (wa_codes, wa_planes) if e == "a" else (wb_codes, wb_planes)
@@ -169,11 +171,13 @@ def tile_list_experts_shared_pl_kernel(tc, xq_words, xq_scales, ws_words, ws_sca
         sum_banks = [y_banks, shared_banks]
 
         def sum_on_tensor(r, pages):
-            turned, banks = pages_t[r % 2], sum_banks[r % 2]
+            banks = sum_banks[r % 2]
             for h in range(HALVES):
                 add_turned(banks[h], [shared_t[4 * h + i][:, r, :] for i in range(4)], True, False)
+            for i, page in enumerate(pages):
+                for h in range(HALVES):
+                    add_turned(turn_banks[h], page_blocks(page, h), i == 0, i == len(pages) - 1)
             for h in range(HALVES):
-                add_turned(turn_banks[h], [b for page in pages for b in page_blocks(page, h)], True, True)
                 nc.scalar.copy(out=turned[h][:], in_=turn_banks[h][:])
             for h in range(HALVES):
                 add_turned(banks[h], [turned[h][:, P * i:P * (i + 1)] for i in range(4)], False, True)
@@ -194,44 +198,37 @@ def tile_list_experts_shared_pl_kernel(tc, xq_words, xq_scales, ws_words, ws_sca
             copy(out=y_bf[c][:, :, 2 * u:2 * u + 2],
                  in_=y_pairs[u][h][:, :, c0:c0 + CHUNK].rearrange("p r t -> p t r"))
 
-        cast_wa(0, 0)
-        cast_wa(0, 1)
-        expert_product("b", 0, expert_banks[0], first_src[:])
-        scatter("b", page_b[0], first_src[:])
-        cast_wa(1, 0)
-        cast_wa(1, 1)
-        page_a = [tile([P, T], F32, "page_a0", tag="wa_raw01"), tile([P, T], F32, "page_a1", tag="wa_raw10")]
-        for page in page_a:
-            nc.gpsimd.memset(page[:], 0.0)
+        for z in range(PASSES):
+            for u in range(2):
+                cast_wa(z, u)
         nc.vector.quantize_mx(out=wa_codes[:].rearrange("p z r m -> p (z r m)").bitcast(FP8X4),
                               scales=wa_planes[:].rearrange("p z r m -> p (z r m)"),
                               in_=wa_bf[:].rearrange("p z r m j -> p (z r m j)"))
-        second_src = wa_raw[1][1][:].rearrange("p j n -> p (j n)")[:, 0:J]
-        expert_product("b", 1, expert_banks[1], second_src)
-        scatter("b", page_b[1], second_src)
+        src_b = [wa_raw[1][1][:].rearrange("p j n -> p (j n)")[:, 0:J]] + [src[:] for src in later_src_b]
+        expert_product("b", 0, expert_banks[0], src_b[0])
+        scatter("b", page_b[0], src_b[0])
+        page_b.append(tile([P, T], F32, "page_b1", tag="wa_raw11"))
+        nc.gpsimd.memset(page_b[1][:], 0.0)
+        expert_product("a", 0, expert_banks[1], src_a[0][:])
         spread_gate("a", y_banks[1])
-        expert_product("a", 0, expert_banks[0], src_ring[0][:])
-        expert_product("a", 1, expert_banks[1], src_ring[1][:])
+        scatter("a", page_a, src_a[0][:])
+        expert_product("b", 1, expert_banks[1], src_b[1])
         for b in range(T // P):
             shared_product(b)
-        scatter("a", page_a[0], src_ring[0][:])
-        scatter("a", page_a[1], src_ring[1][:])
-        expert_product("b", 2, turn_banks[1], src_ring[0][:])
-        finish_slice(0, [page_a[0], page_b[0]])
-        scatter("b", page_b[0], src_ring[0][:])
-        expert_product("a", 2, expert_banks[1], pages_t[0][1][:])
-        finish_slice(1, [page_a[1], page_b[1]])
-        scatter("a", page_a[0], pages_t[0][1][:])
-        expert_product("b", 3, expert_banks[0], pages_t[1][1][:])
-        for c in range(CHUNKS):
-            cast_pair(nc.scalar.copy, 0, c)
-        scatter("b", page_b[1], pages_t[1][1][:])
-        expert_product("a", 3, expert_banks[0], src_ring[1][:])
-        finish_slice(2, [page_a[0], page_b[0]])
-        scatter("a", page_a[1], src_ring[1][:])
+        expert_product("a", 1, expert_banks[1], src_a[1][:])
+        for r in range(1, PACK):
+            scatter("b", page_b[r % 2], src_b[r])
+            finish_slice(r - 1, [page_b[(r - 1) % 2], page_a])
+            scatter("a", page_a, src_a[r][:])
+            if r + 1 < PACK:
+                expert_product("b", r + 1, turn_banks[0], src_b[r + 1])
+                expert_product("a", r + 1, turn_banks[1], src_a[r + 1][:])
+            if r == 2:
+                for c in range(CHUNKS):
+                    cast_pair(nc.scalar.copy, 0, c)
         sum_on_tensor(3, [page_b[1]])
         for h in range(HALVES):
-            nc.vector.tensor_tensor(y_pairs[1][h][:, 1, :], sum_banks[1][h][:], page_a[1][:, BANK * h:BANK * (h + 1)], ADD)
+            nc.vector.tensor_tensor(y_pairs[1][h][:, 1, :], sum_banks[1][h][:], page_a[:, BANK * h:BANK * (h + 1)], ADD)
             store_y(3, h)
         for c in range(CHUNKS):
             cast_pair(nc.scalar.copy if c < 2 else nc.vector.tensor_copy, 1, c)

@@ -58,7 +58,7 @@ def tile_list_experts_shared_pl_kernel(tc, xq_words, xq_scales, ws_words, ws_sca
         wa_planes = tile([P, PASSES, PACK, P], U8, "wa_planes")
         picked = {e: [tile([P, J], U16, f"picked_{e}{z}") for z in range(PASSES)] for e in "ab"}
         picked_scales = {e: tile([P, J], U8, f"picked_scales_{e}") for e in "ab"}
-        picked_scales1 = {"a": tile([P, J], U8, "picked_scales1_a")}
+        picked_scales1 = {e: tile([P, J], U8, f"picked_scales1_{e}") for e in "ab"}
         gate_cols = {e: tile([P, PACK], F32, f"gate_cols_{e}") for e in "ab"}
         gates = {e: tile([P, J], F32, f"gates_{e}") for e in "ab"}
         ident = tile([P, P], F32, "ident")
@@ -68,7 +68,7 @@ def tile_list_experts_shared_pl_kernel(tc, xq_words, xq_scales, ws_words, ws_sca
         shared_t = [tile([P, PACK, P], F32, f"shared_t{b}") for b in range(T // P)]
         turned = [tile([P, BANK], F32, f"turned{h}") for h in range(HALVES)]
         y_pairs = [[tile([P, 2, BANK], F32, f"y{u}{h}") for h in range(HALVES)] for u in range(2)]
-        y_bf = [tile([P, CHUNK, PACK], BF16, f"y_bf{c}") for c in range(CHUNKS)]
+        y_bf = [tile([P, BANK, PACK], BF16, "y_bf0")]
         y_codes = [tile([P, CHUNK], I32, f"y_codes{c}") for c in range(CHUNKS)]
         y_planes = tile([P, T], U8, "y_planes")
 
@@ -79,11 +79,12 @@ def tile_list_experts_shared_pl_kernel(tc, xq_words, xq_scales, ws_words, ws_sca
 
         zero_bytes(nc.vector, x_scales[:])
         zero_bytes(nc.vector, wb_raw_scales[:].rearrange("p z n -> p (z n)"))
-        page_a = tile([P, T], F32, "page_a")
+        page_a = [tile([P, T], F32, "page_a0")]
         nc.vector.memset(page_b[0][:], 0.0)
-        nc.vector.memset(page_a[:], 0.0)
+        nc.vector.memset(page_a[0][:], 0.0)
+        for e in "ba":
+            zero_bytes(nc.gpsimd, picked_scales1[e][:])
         make_identity(nc, ident[:])
-        zero_bytes(nc.gpsimd, picked_scales1["a"][:])
         zero_bytes(nc.gpsimd, ws_planes[:].rearrange("p z n -> p (z n)"))
         zero_bytes(nc.gpsimd, x_scales1[:])
 
@@ -92,7 +93,13 @@ def tile_list_experts_shared_pl_kernel(tc, xq_words, xq_scales, ws_words, ws_sca
                 nc.sync.dma_start(out=plane[32 * q:32 * q + 4, :, :].bitcast(I32),
                                   in_=scales[:, 4 * q:4 * q + 4, :].rearrange("z r n -> r z n").bitcast(I32))
 
-        nc.sync.dma_start(out=gate_cols["b"][:], in_=gb.rearrange("o (p c) -> (o p) c", c=PACK))
+        def load_gate(e, gate):
+            nc.gpsimd.dma_start(out=gate_cols[e][:], in_=gate.rearrange("o (p c) -> (o p) c", c=PACK))
+
+        def load_wa(z, u):
+            rows = wa[512 * z:512 * (z + 1), :].rearrange("(p j) n -> p j n", j=PACK)
+            nc.sync.dma_start(out=wa_raw[z][u][:], in_=rows[:, :, 256 * u:256 * (u + 1)])
+
         nc.sync.dma_start(list_b[:], offs2)
         for q in range(4):
             nc.sync.dma_start(out=x_scales[32 * q:32 * q + 8, :].bitcast(I32),
@@ -103,18 +110,18 @@ def tile_list_experts_shared_pl_kernel(tc, xq_words, xq_scales, ws_words, ws_sca
         load_planes(wb_raw_scales, wb_scales)
         nc.sync.dma_start(list_a[:], offs)
         for z in range(PASSES):
-            rows = wa[512 * z:512 * (z + 1), :].rearrange("(p j) n -> p j n", j=PACK)
             for u in range(2):
-                nc.sync.dma_start(out=wa_raw[z][u][:], in_=rows[:, :, 256 * u:256 * (u + 1)])
-        nc.sync.dma_start(out=gate_cols["a"][:], in_=ga.rearrange("o (p c) -> (o p) c", c=PACK))
+                load_wa(z, u)
+        load_gate("b", gb)
+        load_gate("a", ga)
         nc.sync.dma_start(out=ws_codes[:], in_=ws_words.rearrange("z p n t -> p z (n t)").bitcast(I32))
         load_planes(ws_planes, ws_scales)
         nc.sync.dma_start(out=x_scales1[0:LIVE, :].bitcast(I32), in_=x_scales[4:4 + LIVE, :].bitcast(I32))
 
-        def gather(e, offsets, queue):
+        def gather(e, offsets):
             nc.vector.tensor_copy(picked_scales[e][:], x_scales[:].indirect(offsets[:]))
-            queue.dma_start(out=picked_scales1[e][0:LIVE, :].bitcast(I32),
-                            in_=picked_scales[e][4:4 + LIVE, :].bitcast(I32))
+            nc.gpsimd.dma_start(out=picked_scales1[e][0:LIVE, :].bitcast(I32),
+                                in_=picked_scales[e][4:4 + LIVE, :].bitcast(I32))
             for z in range(PASSES):
                 nc.vector.tensor_copy(picked[e][z][:], x_words[z][:].indirect(offsets[:]))
 
@@ -124,15 +131,12 @@ def tile_list_experts_shared_pl_kernel(tc, xq_words, xq_scales, ws_words, ws_sca
             nc.scalar.copy(out=gates[e][:].rearrange("p (n c) -> p n c", c=PACK),
                            in_=bank[:].rearrange("p (c n) -> p n c", c=PACK))
 
-        spread_gate("b", y_banks[0])
-        picked_scales1["b"] = tile([P, J], U8, "picked_scales1_b", tag="gate_cols_b")
-        zero_bytes(nc.gpsimd, picked_scales1["b"][:])
-        gather("b", list_b, nc.scalar)
+        gather("b", list_b)
         nc.vector.tensor_copy(out=wb_codes[:].rearrange("p z r m -> p z m r"),
                               in_=wb_raw[:].rearrange("p z (m r) -> p z m r", r=PACK))
         nc.vector.tensor_copy(out=wb_planes[:].rearrange("p z r m -> p z m r"),
                               in_=wb_raw_scales[:].rearrange("p z (m r) -> p z m r", r=PACK))
-        gather("a", list_a, nc.sync)
+        gather("a", list_a)
 
         def expert_product(e, r, bank, src):
             codes, planes = (wa_codes, wa_planes) if e == "a" else (wb_codes, wb_planes)
@@ -195,7 +199,7 @@ def tile_list_experts_shared_pl_kernel(tc, xq_words, xq_scales, ws_words, ws_sca
 
         def cast_pair(copy, u, c):
             h, c0 = divmod(c * CHUNK, BANK)
-            copy(out=y_bf[c][:, :, 2 * u:2 * u + 2],
+            copy(out=y_bf[h][:, c0:c0 + CHUNK, 2 * u:2 * u + 2],
                  in_=y_pairs[u][h][:, :, c0:c0 + CHUNK].rearrange("p r t -> p t r"))
 
         for z in range(PASSES):
@@ -206,36 +210,42 @@ def tile_list_experts_shared_pl_kernel(tc, xq_words, xq_scales, ws_words, ws_sca
                               in_=wa_bf[:].rearrange("p z r m j -> p (z r m j)"))
         src_b = [wa_raw[1][1][:].rearrange("p j n -> p (j n)")[:, 0:J]] + [src[:] for src in later_src_b]
         expert_product("b", 0, expert_banks[0], src_b[0])
+        spread_gate("b", y_banks[0])
         scatter("b", page_b[0], src_b[0])
         page_b.append(tile([P, T], F32, "page_b1", tag="wa_raw11"))
         nc.gpsimd.memset(page_b[1][:], 0.0)
         expert_product("a", 0, expert_banks[1], src_a[0][:])
         spread_gate("a", y_banks[1])
-        scatter("a", page_a, src_a[0][:])
+        scatter("a", page_a[0], src_a[0][:])
+        page_a.append(tile([P, T], F32, "page_a1", tag="src_a0"))
+        nc.gpsimd.memset(page_a[1][:], 0.0)
         expert_product("b", 1, expert_banks[1], src_b[1])
         for b in range(T // P):
             shared_product(b)
         expert_product("a", 1, expert_banks[1], src_a[1][:])
         for r in range(1, PACK):
             scatter("b", page_b[r % 2], src_b[r])
-            finish_slice(r - 1, [page_b[(r - 1) % 2], page_a])
-            scatter("a", page_a, src_a[r][:])
+            finish_slice(r - 1, [page_b[(r - 1) % 2], page_a[(r - 1) % 2]])
+            scatter("a", page_a[r % 2], src_a[r][:])
             if r + 1 < PACK:
                 expert_product("b", r + 1, turn_banks[0], src_b[r + 1])
                 expert_product("a", r + 1, turn_banks[1], src_a[r + 1][:])
             if r == 2:
-                for c in range(CHUNKS):
+                for c in range(CHUNKS // 2):
                     cast_pair(nc.scalar.copy, 0, c)
         sum_on_tensor(3, [page_b[1]])
+        y_bf.append(tile([P, BANK, PACK], BF16, "y_bf1", tag="wa_raw11"))
+        for c in range(CHUNKS // 2, CHUNKS):
+            cast_pair(nc.scalar.copy, 0, c)
         for h in range(HALVES):
-            nc.vector.tensor_tensor(y_pairs[1][h][:, 1, :], sum_banks[1][h][:], page_a[:, BANK * h:BANK * (h + 1)], ADD)
+            nc.vector.tensor_tensor(y_pairs[1][h][:, 1, :], sum_banks[1][h][:], page_a[1][:, BANK * h:BANK * (h + 1)], ADD)
             store_y(3, h)
         for c in range(CHUNKS):
-            cast_pair(nc.scalar.copy if c < 2 else nc.vector.tensor_copy, 1, c)
+            cast_pair(nc.scalar.copy if c % 2 == 0 else nc.vector.tensor_copy, 1, c)
         words = out_1[0].rearrange("p c t -> p (c t)").bitcast(I32)
-        for c in (0, 2, 1, 3):
+        for c in (0, 1, 3, 2):
             nc.vector.quantize_mx(out=y_codes[c][:].bitcast(FP8X4), scales=y_planes[:, CHUNK * c:CHUNK * (c + 1)],
-                                  in_=y_bf[c][:].rearrange("p t r -> p (t r)"))
+                                  in_=y_bf[c // 2][:, CHUNK * (c % 2):CHUNK * (c % 2 + 1), :].rearrange("p t r -> p (t r)"))
             nc.sync.dma_start(out=words[:, CHUNK * c:CHUNK * (c + 1)], in_=y_codes[c][:])
         for q in range(4):
             queue = nc.scalar if q % 2 == 0 else nc.sync

@@ -79,14 +79,13 @@ def tile_list_experts_shared_pl_kernel(tc, xq_words, xq_scales, ws_words, ws_sca
 
         zero_bytes(nc.vector, x_scales[:])
         zero_bytes(nc.vector, wb_raw_scales[:].rearrange("p z n -> p (z n)"))
-        page_a = [tile([P, T], F32, "page_a0")]
-        nc.vector.memset(page_b[0][:], 0.0)
-        nc.vector.memset(page_a[0][:], 0.0)
         for e in "ba":
-            zero_bytes(nc.gpsimd, picked_scales1[e][:])
-        make_identity(nc, ident[:])
-        zero_bytes(nc.gpsimd, ws_planes[:].rearrange("p z n -> p (z n)"))
-        zero_bytes(nc.gpsimd, x_scales1[:])
+            zero_bytes(nc.vector, picked_scales1[e][:])
+        zero_bytes(nc.vector, ws_planes[:].rearrange("p z n -> p (z n)"))
+        zero_bytes(nc.vector, x_scales1[:])
+        nc.vector.memset(page_b[0][:], 0.0)
+        nc.vector.memset(ident[:], 0.0)
+        make_identity(nc, ident[:], nomemset=True)
 
         def load_planes(plane, scales):
             for q in range(4):
@@ -132,10 +131,10 @@ def tile_list_experts_shared_pl_kernel(tc, xq_words, xq_scales, ws_words, ws_sca
                            in_=bank[:].rearrange("p (c n) -> p n c", c=PACK))
 
         gather("b", list_b)
-        nc.vector.tensor_copy(out=wb_codes[:].rearrange("p z r m -> p z m r"),
-                              in_=wb_raw[:].rearrange("p z (m r) -> p z m r", r=PACK))
-        nc.vector.tensor_copy(out=wb_planes[:].rearrange("p z r m -> p z m r"),
-                              in_=wb_raw_scales[:].rearrange("p z (m r) -> p z m r", r=PACK))
+        nc.vector.tensor_copy(out=wb_codes[:].rearrange("p z r (b i) -> p z b r i", i=4),
+                              in_=wb_raw[:].rearrange("p z (b i r) -> p z b r i", i=4, r=PACK))
+        nc.vector.tensor_copy(out=wb_planes[:].rearrange("p z r (b i) -> p z b r i", i=16),
+                              in_=wb_raw_scales[:].rearrange("p z (b i r) -> p z b r i", i=16, r=PACK))
         gather("a", list_a)
 
         def expert_product(e, r, bank, src):
@@ -208,6 +207,8 @@ def tile_list_experts_shared_pl_kernel(tc, xq_words, xq_scales, ws_words, ws_sca
         nc.vector.quantize_mx(out=wa_codes[:].rearrange("p z r m -> p (z r m)").bitcast(FP8X4),
                               scales=wa_planes[:].rearrange("p z r m -> p (z r m)"),
                               in_=wa_bf[:].rearrange("p z r m j -> p (z r m j)"))
+        page_a = [tile([P, T], F32, "page_a0", tag="wa_bf")]
+        nc.gpsimd.memset(page_a[0][:], 0.0)
         src_b = [wa_raw[1][1][:].rearrange("p j n -> p (j n)")[:, 0:J]] + [src[:] for src in later_src_b]
         expert_product("b", 0, expert_banks[0], src_b[0])
         spread_gate("b", y_banks[0])

from contextlib import ExitStack

import concourse.mybir as mybir
from concourse.masks import make_identity

K, T, J, N = 1024, 1024, 512, 512
FLOPS = 2 * K * N * (T + 2 * J)

F32 = mybir.dt.float32
BF16 = mybir.dt.bfloat16
I32 = mybir.dt.int32
U16 = mybir.dt.uint16
U8 = mybir.dt.uint8
FP8X4 = mybir.dt.float8_e4m3fn_x4
FP4X4 = mybir.dt.float4_e2m1fn_x4
MULT = mybir.AluOpType.mult
ADD = mybir.AluOpType.add

P = 128
PACK = 4
PASSES = K // 512
BANK = 512
HALVES = T // BANK
CHUNK = 256
CHUNKS = T // CHUNK
LIVE = 100


def tile_list_experts_shared_pl_kernel(tc, xq_words, xq_scales, ws_words, ws_scales, wa, wb_words, wb_scales,
                                           ga, gb, offs, offs2, out_0, out_1, out_2):
    nc = tc.nc
    with ExitStack() as ctx:
        lists = ctx.enter_context(tc.tile_pool(name="lists", bufs=1))
        sb = ctx.enter_context(tc.tile_pool(name="sb", bufs=1))
        ps = ctx.enter_context(tc.psum_pool(name="ps", bufs=1))

        def tile(shape, dtype, name, tag=None):
            return sb.tile(shape, dtype, name=name, tag=tag or name, align_bytes=64)

        def zero_bytes(engine, plane):
            engine.memset(plane.bitcast(I32), 0)

        list_a = lists.tile([P, J // 16], U16, name="list_a")
        list_b = lists.tile([P, J // 16], U16, name="list_b")

        x_words = [tile([P, T], U16, f"x_words{z}") for z in range(PASSES)]
        x_scales = tile([P, T], U8, "x_scales")
        x_scales1 = tile([P, T], U8, "x_scales1")
        wb_raw = tile([P, PASSES, N], I32, "wb_raw")
        wb_raw_scales = tile([P, PASSES, N], U8, "wb_raw_scales")
        wb_codes = tile([P, PASSES, PACK, P], I32, "wb_codes")
        wb_planes = tile([P, PASSES, PACK, P], U8, "wb_planes")
        ws_codes = tile([P, PASSES, N], I32, "ws_codes")
        ws_planes = tile([P, PASSES, N], U8, "ws_planes")
        wa_raw = [[tile([P, PACK, N // 2], F32, f"wa_raw{z}{u}") for u in range(2)] for z in range(PASSES)]
        wa_bf = tile([P, PASSES, PACK, P, PACK], BF16, "wa_bf")
        wa_codes = tile([P, PASSES, PACK, P], I32, "wa_codes")
        wa_planes = tile([P, PASSES, PACK, P], U8, "wa_planes")
        picked = {e: [tile([P, J], U16, f"picked_{e}{z}") for z in range(PASSES)] for e in "ab"}
        picked_scales = {e: tile([P, J], U8, f"picked_scales_{e}") for e in "ab"}
        picked_scales1 = {e: tile([P, J], U8, f"picked_scales1_{e}") for e in "ab"}
        gate_cols = {e: tile([P, PACK], F32, f"gate_cols_{e}") for e in "ab"}
        gates = {e: tile([P, J], F32, f"gates_{e}") for e in "ab"}
        ident = tile([P, P], F32, "ident")
        page_b = [tile([P, T], F32, "page_b0")]
        src_a = [tile([P, J], F32, f"src_a{r}") for r in range(PACK)]
        later_src_b = [tile([P, J], F32, f"src_b{r}") for r in range(1, PACK)]
        shared_t = [tile([P, PACK, P], F32, f"shared_t{b}") for b in range(T // P)]
        turned = [tile([P, BANK], F32, f"turned{h}") for h in range(HALVES)]
        y_pairs = [[tile([P, 2, BANK], F32, f"y{u}{h}") for h in range(HALVES)] for u in range(2)]
        y_bf = [tile([P, BANK, PACK], BF16, "y_bf0")]
        y_codes = [tile([P, CHUNK], I32, f"y_codes{c}") for c in range(CHUNKS)]
        y_planes = tile([P, T], U8, "y_planes")

        expert_banks = [ps.tile([P, BANK], F32, name=f"expert_bank{i}") for i in range(2)]
        shared_banks = [ps.tile([P, BANK], F32, name=f"shared_bank{i}") for i in range(2)]
        turn_banks = [ps.tile([P, BANK], F32, name=f"turn_bank{h}") for h in range(HALVES)]
        y_banks = [ps.tile([P, BANK], F32, name=f"y_bank{h}") for h in range(HALVES)]

        zero_bytes(nc.vector, x_scales[:])
        zero_bytes(nc.vector, wb_raw_scales[:].rearrange("p z n -> p (z n)"))
        for e in "ba":
            zero_bytes(nc.vector, picked_scales1[e][:])
        zero_bytes(nc.vector, ws_planes[:].rearrange("p z n -> p (z n)"))
        zero_bytes(nc.vector, x_scales1[:])
        nc.vector.memset(page_b[0][:], 0.0)
        nc.vector.memset(ident[:], 0.0)
        make_identity(nc, ident[:], nomemset=True)

        def load_planes(plane, scales):
            for q in range(4):
                nc.sync.dma_start(out=plane[32 * q:32 * q + 4, :, :].bitcast(I32),
                                  in_=scales[:, 4 * q:4 * q + 4, :].rearrange("z r n -> r z n").bitcast(I32))

        def load_gate(e, gate):
            nc.gpsimd.dma_start(out=gate_cols[e][:], in_=gate.rearrange("o (p c) -> (o p) c", c=PACK))

        def load_wa(z, u):
            rows = wa[512 * z:512 * (z + 1), :].rearrange("(p j) n -> p j n", j=PACK)
            nc.sync.dma_start(out=wa_raw[z][u][:], in_=rows[:, :, 256 * u:256 * (u + 1)])

        nc.sync.dma_start(list_b[:], offs2)
        for q in range(4):
            nc.sync.dma_start(out=x_scales[32 * q:32 * q + 8, :].bitcast(I32),
                              in_=xq_scales[:, 4 * q:4 * q + 4, :].bitcast(I32))
        for z in range(PASSES):
            nc.sync.dma_start(out=x_words[z][:].bitcast(I32), in_=xq_words[z].bitcast(I32))
        nc.sync.dma_start(out=wb_raw[:], in_=wb_words.rearrange("z p n t -> p z (n t)").bitcast(I32))
        load_planes(wb_raw_scales, wb_scales)
        nc.sync.dma_start(list_a[:], offs)
        for z in range(PASSES):
            for u in range(2):
                load_wa(z, u)
        load_gate("b", gb)
        load_gate("a", ga)
        nc.sync.dma_start(out=ws_codes[:], in_=ws_words.rearrange("z p n t -> p z (n t)").bitcast(I32))
        load_planes(ws_planes, ws_scales)
        nc.sync.dma_start(out=x_scales1[0:LIVE, :].bitcast(I32), in_=x_scales[4:4 + LIVE, :].bitcast(I32))

        def gather(e, offsets):
            nc.vector.tensor_copy(picked_scales[e][:], x_scales[:].indirect(offsets[:]))
            nc.gpsimd.dma_start(out=picked_scales1[e][0:LIVE, :].bitcast(I32),
                                in_=picked_scales[e][4:4 + LIVE, :].bitcast(I32))
            for z in range(PASSES):
                nc.vector.tensor_copy(picked[e][z][:], x_words[z][:].indirect(offsets[:]))

        def spread_gate(e, bank):
            for c in range(PACK):
                nc.tensor.transpose(bank[:, P * c:P * (c + 1)], gate_cols[e][:, c:c + 1].to_broadcast([P, P]), ident[:])
            nc.scalar.copy(out=gates[e][:].rearrange("p (n c) -> p n c", c=PACK),
                           in_=bank[:].rearrange("p (c n) -> p n c", c=PACK))

        gather("b", list_b)
        nc.vector.tensor_copy(out=wb_codes[:].rearrange("p z r (b i) -> p z b r i", i=4),
                              in_=wb_raw[:].rearrange("p z (b i r) -> p z b r i", i=4, r=PACK))
        nc.vector.tensor_copy(out=wb_planes[:].rearrange("p z r (b i) -> p z b r i", i=16),
                              in_=wb_raw_scales[:].rearrange("p z (b i r) -> p z b r i", i=16, r=PACK))
        gather("a", list_a)

        def expert_product(e, r, bank, src):
            codes, planes = (wa_codes, wa_planes) if e == "a" else (wb_codes, wb_planes)
            for z in range(PASSES):
                nc.tensor.matmul_mx(out=bank[:], lhsT=codes[:, z, r, :].bitcast(FP8X4), lhsT_scale=planes[:, z, r, :],
                                    rhs=picked[e][z][:].bitcast(FP4X4),
                                    rhs_scale=(picked_scales, picked_scales1)[z][e][:],
                                    start=z == 0, stop=z == PASSES - 1)
            nc.scalar.copy(out=src, in_=bank[:])

        def scatter(e, page, src):
            offsets = list_a if e == "a" else list_b
            nc.vector.tensor_tensor(page[:].indirect(offsets[:]), src, gates[e][:], MULT)

        def cast_wa(z, u):
            nc.scalar.copy(out=wa_bf[:, z, :, 64 * u:64 * (u + 1), :].rearrange("p r m j -> p m j r"),
                           in_=wa_raw[z][u][:].rearrange("p j (m r) -> p m j r", r=PACK))

        def shared_product(b):
            bank = (shared_banks + turn_banks)[b % 4]
            for z in range(PASSES):
                nc.tensor.matmul_mx(out=bank[:], lhsT=x_words[z][:, P * b:P * (b + 1)].bitcast(FP4X4),
                                    lhsT_scale=(x_scales, x_scales1)[z][:, P * b:P * (b + 1)],
                                    rhs=ws_codes[:, z, :].bitcast(FP8X4), rhs_scale=ws_planes[:, z, :],
                                    start=z == 0, stop=z == PASSES - 1)
            nc.scalar.copy(out=shared_t[b][:], in_=bank[:].rearrange("p (m r) -> p r m", r=PACK))

        def add_turned(bank, blocks, start, stop):
            for i, block in enumerate(blocks):
                nc.tensor.matmul(bank[:, P * (i % 4):P * (i % 4 + 1)], lhsT=block, rhs=ident[:], is_transpose=True,
                                 start=start and i == 0, stop=stop and i == len(blocks) - 1)

        def page_blocks(page, h):
            return [page[:, BANK * h + P * i:BANK * h + P * (i + 1)] for i in range(4)]

        sum_banks = [y_banks, shared_banks]

        def sum_on_tensor(r, pages):
            banks = sum_banks[r % 2]
            for h in range(HALVES):
                add_turned(banks[h], [shared_t[4 * h + i][:, r, :] for i in range(4)], True, False)
            for i, page in enumerate(pages):
                for h in range(HALVES):
                    add_turned(turn_banks[h], page_blocks(page, h), i == 0, i == len(pages) - 1)
            for h in range(HALVES):
                nc.scalar.copy(out=turned[h][:], in_=turn_banks[h][:])
            for h in range(HALVES):
                add_turned(banks[h], [turned[h][:, P * i:P * (i + 1)] for i in range(4)], False, True)

        y_rows = out_0.rearrange("(p r) t -> r p t", r=PACK)

        def store_y(r, h):
            nc.sync.dma_start(out=y_rows[r][:, BANK * h:BANK * (h + 1)], in_=y_pairs[r // 2][h][:, r % 2, :])

        def finish_slice(r, pages):
            sum_on_tensor(r, pages)
            for h in range(HALVES):
                nc.scalar.copy(out=y_pairs[r // 2][h][:, r % 2, :], in_=sum_banks[r % 2][h][:])
                store_y(r, h)

        def cast_pair(copy, u, c):
            h, c0 = divmod(c * CHUNK, BANK)
            copy(out=y_bf[h][:, c0:c0 + CHUNK, 2 * u:2 * u + 2],
                 in_=y_pairs[u][h][:, :, c0:c0 + CHUNK].rearrange("p r t -> p t r"))

        for z in range(PASSES):
            for u in range(2):
                cast_wa(z, u)
        nc.vector.quantize_mx(out=wa_codes[:].rearrange("p z r m -> p (z r m)").bitcast(FP8X4),
                              scales=wa_planes[:].rearrange("p z r m -> p (z r m)"),
                              in_=wa_bf[:].rearrange("p z r m j -> p (z r m j)"))
        page_a = [tile([P, T], F32, "page_a0", tag="wa_bf")]
        nc.gpsimd.memset(page_a[0][:], 0.0)
        src_b = [wa_raw[1][1][:].rearrange("p j n -> p (j n)")[:, 0:J]] + [src[:] for src in later_src_b]
        expert_product("b", 0, expert_banks[0], src_b[0])
        spread_gate("b", y_banks[0])
        scatter("b", page_b[0], src_b[0])
        page_b.append(tile([P, T], F32, "page_b1", tag="wa_raw11"))
        nc.gpsimd.memset(page_b[1][:], 0.0)
        expert_product("a", 0, expert_banks[1], src_a[0][:])
        spread_gate("a", y_banks[1])
        scatter("a", page_a[0], src_a[0][:])
        page_a.append(tile([P, T], F32, "page_a1", tag="src_a0"))
        nc.gpsimd.memset(page_a[1][:], 0.0)
        expert_product("b", 1, expert_banks[1], src_b[1])
        for b in range(T // P):
            shared_product(b)
        expert_product("a", 1, expert_banks[1], src_a[1][:])
        for r in range(1, PACK):
            scatter("b", page_b[r % 2], src_b[r])
            finish_slice(r - 1, [page_b[(r - 1) % 2], page_a[(r - 1) % 2]])
            scatter("a", page_a[r % 2], src_a[r][:])
            if r + 1 < PACK:
                expert_product("b", r + 1, turn_banks[0], src_b[r + 1])
                expert_product("a", r + 1, turn_banks[1], src_a[r + 1][:])
            if r == 2:
                for c in range(CHUNKS // 2):
                    cast_pair(nc.scalar.copy, 0, c)
        sum_on_tensor(3, [page_b[1]])
        y_bf.append(tile([P, BANK, PACK], BF16, "y_bf1", tag="wa_raw11"))
        for c in range(CHUNKS // 2, CHUNKS):
            cast_pair(nc.scalar.copy, 0, c)
        for h in range(HALVES):
            nc.vector.tensor_tensor(y_pairs[1][h][:, 1, :], sum_banks[1][h][:], page_a[1][:, BANK * h:BANK * (h + 1)], ADD)
            store_y(3, h)
        for c in range(CHUNKS):
            cast_pair(nc.scalar.copy if c % 2 == 0 else nc.vector.tensor_copy, 1, c)
        words = out_1[0].rearrange("p c t -> p (c t)").bitcast(I32)
        for c in (0, 1, 3, 2):
            nc.vector.quantize_mx(out=y_codes[c][:].bitcast(FP8X4), scales=y_planes[:, CHUNK * c:CHUNK * (c + 1)],
                                  in_=y_bf[c // 2][:, CHUNK * (c % 2):CHUNK * (c % 2 + 1), :].rearrange("p t r -> p (t r)"))
            nc.sync.dma_start(out=words[:, CHUNK * c:CHUNK * (c + 1)], in_=y_codes[c][:])
        for q in range(4):
            queue = nc.scalar if q % 2 == 0 else nc.sync
            queue.dma_start(out=out_2[0, 4 * q:4 * q + 4, :].bitcast(I32),
                            in_=y_planes[32 * q:32 * q + 4, :].bitcast(I32))
